import numpy as np
import ml_dtypes


def mxq(x, axis, fmt="e4m3"):
    dtype, down = {"e4m3": (ml_dtypes.float8_e4m3fn, 7), "e5m2": (ml_dtypes.float8_e5m2, 14)}[fmt]
    v = np.moveaxis(np.asarray(x, np.float32).astype(ml_dtypes.bfloat16).astype(np.float64), axis, -1)
    blocks = v.reshape(v.shape[:-1] + (-1, 32))
    amax = np.abs(blocks).max(-1, keepdims=True)
    byte = np.maximum(np.where(amax > 0, np.frexp(amax)[1] - 1 + 127, 0) - down, 1)
    scale = np.exp2(byte - 127.0)
    codes = (blocks / scale).astype(np.float32).astype(dtype).astype(np.float64)
    return np.moveaxis((codes * scale).reshape(v.shape), -1, axis)


WIDE = False


def mx_kscale(k):
    if not WIDE:
        return np.ones(k)
    levels = np.array([10, -10, 5, -5, 0])
    if k % 512:
        return np.exp2(np.random.permutation(np.resize(levels, k // 32))).repeat(32)
    a = np.empty((k // 512, 16))
    for p in range(k // 512):
        a[p, :8] = np.random.permutation(np.resize(levels, 8))
        for g in range(8):
            far = levels[np.abs(levels - a[p, g]) >= 10]
            a[p, g + 8] = far[np.random.randint(len(far))]
    return np.exp2(a.ravel()).repeat(32)


def f64(x):
    return np.asarray(x).astype(np.float64)


def striped(idx):
    return np.tile(idx.reshape(-1, 16).T, (8, 1)).astype(np.uint16)


def unstriped(offs):
    return offs[:16].T.reshape(-1).astype(np.int64)


E2M1 = np.array([0.0, 0.5, 1.0, 1.5, 2.0, 3.0, 4.0, 6.0, -0.0, -0.5, -1.0, -1.5, -2.0, -3.0, -4.0, -6.0])


def pack_weight(w, fmt):
    k, n = w.shape
    w = f64(np.asarray(w, np.float32).astype(ml_dtypes.bfloat16)).reshape(k // 32, 32, n)
    amax = np.abs(w).max(1)
    if fmt == "e4m3":
        byte = np.frexp(amax)[1] - 1 + 127 - 7
    else:
        mant, ex = np.frexp(amax / 6.0)
        byte = np.where(mant > 0.5, ex, ex - 1) + 127
    byte = np.clip(np.where(amax > 0, byte, 1), 1, 254)
    scaled = (w * np.exp2(127.0 - byte)[:, None, :]).reshape(k, n).astype(np.float32)
    by_word = np.ascontiguousarray(scaled.reshape(k // 512, 128, 4, n).transpose(0, 1, 3, 2))
    if fmt == "e4m3":
        words = by_word.astype(ml_dtypes.float8_e4m3fn).view(np.uint8)
    else:
        c = by_word.astype(ml_dtypes.float4_e2m1fn).view(np.uint8) & 0xF
        words = (c[..., 0::2] | (c[..., 1::2] << 4)).reshape(k // 512, 128, 2 * n)
    return np.ascontiguousarray(words), np.ascontiguousarray(byte.astype(np.uint8).reshape(k // 512, 16, n))


def unpack_weight(words, scales, fmt):
    g, _, n = scales.shape
    words = np.ascontiguousarray(words).reshape(g, 128, n, -1)
    if fmt == "e4m3":
        vals = words.view(ml_dtypes.float8_e4m3fn).astype(np.float64)
    else:
        nib = np.empty((g, 128, n, 4), np.uint8)
        nib[..., 0::2] = words & 0xF
        nib[..., 1::2] = words >> 4
        vals = E2M1[nib]
    vals = vals * np.repeat(np.exp2(scales.astype(np.float64) - 127.0), 8, axis=1)[..., None]
    return vals.transpose(0, 1, 3, 2).reshape(g * 512, n)


def gelu(v):
    return 0.5 * v * (1.0 + np.tanh(np.sqrt(2.0 / np.pi) * (v + 0.044715 * v**3)))


def bf(x):
    return np.asarray(x, np.float32).astype(ml_dtypes.bfloat16)


def planes(Y):
    n, m = Y.shape
    b = f64(bf(Y)).reshape(n // 32, 32, m)
    amax = np.abs(b).max(1)
    byte = np.clip(np.where(amax > 0, np.frexp(amax)[1] - 1 + 127 - 7, 1), 1, 254)
    codes = (b * np.exp2(127.0 - byte)[:, None, :]).reshape(n, m).astype(np.float32).astype(ml_dtypes.float8_e4m3fn).view(np.uint8)
    words = codes.reshape(n // 512, 128, 4, m).transpose(0, 1, 3, 2)
    return np.ascontiguousarray(words), np.ascontiguousarray(byte.astype(np.uint8).reshape(n // 512, 16, m))


K, K2, H, N, T, S = 1024, 512, 1024, 512, 2048, 1024


def setup_inputs():
    n = np.random.standard_normal
    s = mx_kscale(K)[:, None]
    s2 = mx_kscale(K2)[:, None]
    u = mx_kscale(H)[:, None]
    d = {}
    d["tab_words"], d["tab_scales"] = pack_weight(n((K, T)) * s, "e4m3")
    d["offs"] = striped(np.random.permutation(T)[:S])
    d["xs_words"], d["xs_scales"] = pack_weight(n((K2, S)) * s2, "e4m3")
    d["w1"] = (1.4 * n((K, H)) / K**0.5 / s * u.T).astype(np.float32)
    d["w2_words"], d["w2_scales"] = pack_weight(1.6 * n((K2, H)) / K2**0.5 / s2, "e2m1")
    d["fringe"] = (0.8 * n(H)).astype(np.float32)
    d["gain"] = (0.5 * np.exp(0.3 * n(H)) * u[:, 0]).astype(np.float32)
    d["w3"] = (n((H, N)) / H**0.5 / u * np.exp(0.8 * n(N))).astype(np.float32)
    return d


def reference(tab_words, tab_scales, offs, xs_words, xs_scales, w1, w2_words, w2_scales, fringe, gain, w3):
    v = unpack_weight(tab_words, tab_scales, "e4m3")[:, unstriped(offs)]
    xs = unpack_weight(xs_words, xs_scales, "e4m3")
    w2 = unpack_weight(w2_words, w2_scales, "e2m1")
    a = mxq(f64(w1), 0, "e4m3").T @ v
    b = (w2.T @ xs) + f64(fringe)[:, None]
    z = a / np.sqrt(1.0 + b * b) + f64(gain)[:, None] * b
    zq = mxq(z, 0, "e4m3")
    y = mxq(f64(w3), 0, "e4m3").T @ zq
    words, scales = planes(y)
    return y, words, scales

@@ -1,0 +1,267 @@
+from contextlib import ExitStack
+
+import concourse.mybir as mybir
+
+K, K2, H, N, T, S = 1024, 512, 1024, 512, 2048, 1024
+FLOPS = 2 * S * (K * H + K2 * H + H * N)
+
+F32 = mybir.dt.float32
+BF16 = mybir.dt.bfloat16
+I32 = mybir.dt.int32
+U32 = mybir.dt.uint32
+U16 = mybir.dt.uint16
+U8 = mybir.dt.uint8
+FP8X4 = mybir.dt.float8_e4m3fn_x4
+FP4X4 = mybir.dt.float4_e2m1fn_x4
+ACT = mybir.ActivationFunctionType
+ALU = mybir.AluOpType
+
+P = 128
+PACK = 4
+PASS = P * PACK
+HALF = 512
+CHUNK = 256
+
+
+def tile_list_tyre_shear_features_kernel(
+    tc, tab_words, tab_scales, offs, xs_words, xs_scales, w1, w2_words, w2_scales, fringe, gain, w3,
+    out_0, out_1, out_2,
+):
+    nc = tc.nc
+    with ExitStack() as ctx:
+        keep = ctx.enter_context(tc.tile_pool(name="keep", bufs=1))
+        ring = ctx.enter_context(tc.tile_pool(name="ring", bufs=2))
+        psum = ctx.enter_context(tc.psum_pool(name="psum", bufs=1))
+
+        def held(shape, dtype, name):
+            return keep.tile(shape, dtype, name=name, align_bytes=64)
+
+        offsets = keep.tile([P, S // 16], U16, name="offsets")
+
+        w2_plane = held([P, H], U8, "w2_plane")
+        xs_plane = held([P, S], U8, "xs_plane")
+        tab_plane = held([P, T], U8, "tab_plane")
+        nc.vector.memset(tab_plane[:].bitcast(I32), 0)
+
+        warm_in = held([P, 1], F32, "warm_in")
+        warm_out = held([P, 1], F32, "warm_out")
+        nc.vector.memset(warm_in[:], 1.0)
+        nc.scalar.activation(warm_out[:], warm_in[:], ACT.Abs_reciprocal_sqrt)
+
+        w2_raw = held([P, 2 * H], U8, "w2_raw")
+        def load_quadrant(queue, plane, scales, q):
+            rows = scales[0, 4 * q : 4 * q + 4, :].bitcast(I32)
+            queue.dma_start(
+                plane[32 * q : 32 * q + 32, :].bitcast(I32), rows.unsqueeze(0).broadcast_to([8, 4, rows.shape[1]])
+            )
+
+        for q in range(4):
+            load_quadrant(nc.sync, w2_plane, w2_scales, q)
+        nc.sync.dma_start(w2_raw[:].bitcast(I32), w2_words[0].bitcast(I32))
+        xs_codes = held([P, S], I32, "xs_codes")
+        nc.sync.dma_start(xs_codes[:], xs_words[0].rearrange("p c i -> p (c i)").bitcast(I32))
+        fringe_col = held([P, 2, PACK], F32, "fringe_col")
+        gain_col = held([P, 2, PACK], F32, "gain_col")
+        gf_col = held([P, 2, PACK], F32, "gf_col")
+        for q in range(4):
+            load_quadrant(nc.sync if q < 2 else nc.gpsimd, xs_plane, xs_scales, q)
+        nc.sync.dma_start(fringe_col[:], fringe.rearrange("(b p t) -> p b t", b=2, t=PACK))
+        nc.sync.dma_start(gain_col[:], gain.rearrange("(b p t) -> p b t", b=2, t=PACK))
+        nc.gpsimd.tensor_tensor(gf_col[:], gain_col[:], fringe_col[:], ALU.mult)
+
+        tab_codes = [held([P, T], I32, "tab_codes%d" % a) for a in range(2)]
+        nc.sync.dma_start(tab_codes[0][:], tab_words[0].rearrange("p t i -> p (t i)").bitcast(I32))
+        nc.sync.dma_start(offsets[:], offs)
+        for q in range(4):
+            nc.sync.dma_start(
+                tab_plane[32 * q : 32 * q + 8, :].bitcast(I32), tab_scales[:, 4 * q : 4 * q + 4, :].bitcast(I32)
+            )
+        nc.sync.dma_start(tab_codes[1][:], tab_words[1].rearrange("p t i -> p (t i)").bitcast(I32))
+
+        w1_raw = {}
+        for b in range(2):
+            for a in range(2):
+                raw = held([P, PACK, PASS], F32, "w1_raw%d%d" % (b, a))
+                rows = w1[PASS * a : PASS * (a + 1), PASS * b : PASS * (b + 1)]
+                nc.sync.dma_start(raw[:], rows.rearrange("(p j) c -> p j c", j=PACK))
+                w1_raw[b, a] = raw
+        w3_raw = {}
+        for b in range(2):
+            raw = held([P, PACK, N], F32, "w3_raw%d" % b)
+            nc.sync.dma_start(raw[:], w3[PASS * b : PASS * (b + 1), :].rearrange("(p j) c -> p j c", j=PACK))
+            w3_raw[b] = raw
+
+        w2_codes, w2_dealt = {}, {}
+        for b in range(2):
+            codes = held([P, 2 * PASS], U8, "w2_codes%d" % b)
+            nc.vector.tensor_copy(
+                codes[:].rearrange("p (t q e) -> p q t e", t=PACK, e=2),
+                w2_raw[:, 2 * PASS * b : 2 * PASS * (b + 1)].rearrange("p (q t e) -> p q t e", t=PACK, e=2),
+            )
+            plane = held([P, PASS], U8, "w2_dealt%d" % b)
+            nc.vector.tensor_copy(
+                plane[:].rearrange("p (t q) -> p q t", t=PACK),
+                w2_plane[:, PASS * b : PASS * (b + 1)].rearrange("p (q t) -> p q t", t=PACK),
+            )
+            w2_codes[b], w2_dealt[b] = codes, plane
+
+        damp, resp = {}, {}
+
+        def frame_terms(b, h):
+            cols = slice(HALF * h, HALF * (h + 1))
+            d = held([P, PACK, HALF], F32, "damp%d%d" % (b, h))
+            r = held([P, PACK, HALF], F32, "resp%d%d" % (b, h))
+            for t in range(PACK):
+                bank = psum.tile([P, HALF], F32, name="by_bank", tag="by_bank", bufs=5)
+                nc.tensor.matmul_mx(
+                    out=bank[:],
+                    lhsT=w2_codes[b][:, 2 * P * t : 2 * P * (t + 1)].bitcast(FP4X4),
+                    lhsT_scale=w2_dealt[b][:, P * t : P * (t + 1)],
+                    rhs=xs_codes[:, cols].bitcast(FP8X4),
+                    rhs_scale=xs_plane[:, cols],
+                    start=True,
+                    stop=True,
+                )
+                nc.scalar.activation(d[:, t, :], bank[:], ACT.Square, bias=fringe_col[:, b, t : t + 1])
+                nc.scalar.activation(
+                    r[:, t, :], bank[:], ACT.Identity, bias=gf_col[:, b, t : t + 1], scale=gain_col[:, b, t : t + 1]
+                )
+                if t % 2 == 1:
+                    pair = d[:, t - 1 : t + 1, :]
+                    nc.scalar.activation(pair, pair, ACT.Abs_reciprocal_sqrt, bias=1.0)
+            damp[b, h], resp[b, h] = d, r
+
+        v_codes, v_plane = {}, {}
+
+        def gather(h):
+            picked = offsets[:, (HALF // 16) * h : (HALF // 16) * (h + 1)]
+            for a in range(2):
+                codes = held([P, HALF], U32, "v_codes%d%d" % (a, h))
+                nc.vector.tensor_copy(codes[:], tab_codes[a][:].bitcast(U32).indirect(picked))
+                v_codes[a, h] = codes
+            plane = held([P, HALF], U8, "v_plane%d" % h)
+            nc.vector.tensor_copy(plane[:], tab_plane[:].indirect(picked))
+            v_plane[h] = plane
+
+        def group_weight(raw, on_scalar):
+            grouped = ring.tile([P, PACK * PASS], BF16, name="w_grouped", tag="w_grouped", bufs=4, align_bytes=64)
+            dst = grouped[:].rearrange("p (t q j) -> p q j t", t=PACK, j=PACK)
+            src = raw[:].rearrange("p j (q t) -> p q j t", t=PACK)
+            if on_scalar:
+                nc.scalar.copy(dst, src)
+            else:
+                nc.vector.tensor_copy(dst, src)
+            return grouped
+
+        def quantise_weight(grouped, name):
+            codes = held([P, PASS], U32, name + "_codes")
+            plane = held([P, PASS], U8, name + "_plane")
+            nc.vector.quantize_mx(out=codes[:].bitcast(FP8X4), scales=plane[:], in_=grouped[:])
+            return codes, plane
+
+        w1_q, w3_q = {}, {}
+
+        def prepare_w1(b):
+            grouped = [group_weight(w1_raw[b, a], False) for a in range(2)]
+            for a in range(2):
+                w1_q[b, a] = quantise_weight(grouped[a], "w1_%d%d" % (b, a))
+
+        z_q = {}
+
+        def casing_terms(b, h):
+            d, r = damp[b, h], resp[b, h]
+            for t in range(PACK):
+                bank = psum.tile([P, HALF], F32, name="a_bank", tag="a_bank", bufs=3)
+                for a in range(2):
+                    codes, plane = w1_q[b, a]
+                    nc.tensor.matmul_mx(
+                        out=bank[:],
+                        lhsT=codes[:, P * t : P * (t + 1)].bitcast(FP8X4),
+                        lhsT_scale=plane[:, P * t : P * (t + 1)],
+                        rhs=v_codes[a, h][:].bitcast(FP8X4),
+                        rhs_scale=v_plane[h][4 * a : P, :],
+                        start=(a == 0),
+                        stop=(a == 1),
+                    )
+                nc.vector.tensor_tensor(d[:, t, :], bank[:], d[:, t, :], ALU.mult)
+            grouped = []
+            for c in range(2):
+                cols = slice(CHUNK * c, CHUNK * (c + 1))
+                g = ring.tile([P, PACK * CHUNK], BF16, name="z_grouped", tag="z_grouped", bufs=4, align_bytes=64)
+                nc.vector.tensor_tensor(
+                    g[:].rearrange("p (c i t) -> p c t i", i=4, t=PACK),
+                    d[:, :, cols].rearrange("p t (c i) -> p c t i", i=4),
+                    r[:, :, cols].rearrange("p t (c i) -> p c t i", i=4),
+                    ALU.add,
+                )
+                grouped.append(g)
+            for c in range(2):
+                codes = held([P, CHUNK], U32, "z_codes%d%d%d" % (b, h, c))
+                plane = held([P, CHUNK], U8, "z_plane%d%d%d" % (b, h, c))
+                nc.vector.quantize_mx(out=codes[:].bitcast(FP8X4), scales=plane[:], in_=grouped[c][:])
+                z_q[b, 2 * h + c] = (codes, plane)
+
+        y_plane = held([P, S], U8, "y_plane")
+        out_rows = out_0.rearrange("(p t) j -> p t j", t=PACK)
+        out_words = out_1[0].rearrange("p m t -> p (m t)").bitcast(I32)
+
+        def features(c):
+            cols = slice(CHUNK * c, CHUNK * (c + 1))
+            y = ring.tile([P, PACK, CHUNK], F32, name="y", tag="y", bufs=3, align_bytes=64)
+            for u in range(2):
+                bank = psum.tile([P, 2, CHUNK], F32, name="by_bank", tag="by_bank", bufs=5)
+                for e in range(2):
+                    t = 2 * u + e
+                    for b in range(2):
+                        w_codes, w_plane = w3_q[b]
+                        z_codes, z_plane = z_q[b, c]
+                        nc.tensor.matmul_mx(
+                            out=bank[:, e, :],
+                            lhsT=w_codes[:, P * t : P * (t + 1)].bitcast(FP8X4),
+                            lhsT_scale=w_plane[:, P * t : P * (t + 1)],
+                            rhs=z_codes[:].bitcast(FP8X4),
+                            rhs_scale=z_plane[:],
+                            start=(b == 0),
+                            stop=(b == 1),
+                        )
+                nc.scalar.copy(y[:, 2 * u : 2 * u + 2, :], bank[:])
+            nc.sync.dma_start(out_rows[:, :, cols], y[:])
+            g = ring.tile([P, PACK * CHUNK], BF16, name="y_grouped", tag="y_grouped", align_bytes=64)
+            copy = nc.scalar.copy if c < 2 else nc.vector.tensor_copy
+            copy(
+                g[:].rearrange("p (c i t) -> p c t i", i=4, t=PACK),
+                y[:].rearrange("p t (c i) -> p c t i", i=4),
+            )
+            return g
+
+        def planes(c, g):
+            cols = slice(CHUNK * c, CHUNK * (c + 1))
+            codes = held([P, CHUNK], U32, "y_codes%d" % c)
+            nc.vector.quantize_mx(out=codes[:].bitcast(FP8X4), scales=y_plane[:, cols], in_=g[:])
+            nc.sync.dma_start(out_words[:, cols], codes[:].bitcast(I32))
+
+        frame_terms(0, 0)
+        gather(0)
+        prepare_w1(0)
+        frame_terms(1, 0)
+        gather(1)
+        casing_terms(0, 0)
+        prepare_w1(1)
+        frame_terms(0, 1)
+        casing_terms(1, 0)
+        w3_grouped = [group_weight(w3_raw[b], True) for b in range(2)]
+        frame_terms(1, 1)
+        casing_terms(0, 1)
+        for b in range(2):
+            w3_q[b] = quantise_weight(w3_grouped[b], "w3_%d" % b)
+        first = [features(c) for c in range(2)]
+        casing_terms(1, 1)
+        for c in range(2):
+            planes(c, first[c])
+        last = [features(c) for c in range(2, 4)]
+        for c in range(2, 4):
+            planes(c, last[c - 2])
+        for q in range(4):
+            nc.sync.dma_start(
+                out_2[0, 4 * q : 4 * q + 4, :].bitcast(I32), y_plane[32 * q : 32 * q + 4, :].bitcast(I32)
+            )

@@ -64,10 +64,10 @@ def tile_list_tyre_shear_features_kernel(
         gain_col = held([P, 2, PACK], F32, "gain_col")
         gf_col = held([P, 2, PACK], F32, "gf_col")
         for q in range(4):
-            load_quadrant(nc.sync if q < 2 else nc.gpsimd, xs_plane, xs_scales, q)
-        nc.sync.dma_start(fringe_col[:], fringe.rearrange("(b p t) -> p b t", b=2, t=PACK))
+            load_quadrant(nc.sync, xs_plane, xs_scales, q)
+        nc.gpsimd.dma_start(fringe_col[:], fringe.rearrange("(b p t) -> p b t", b=2, t=PACK))
         nc.sync.dma_start(gain_col[:], gain.rearrange("(b p t) -> p b t", b=2, t=PACK))
-        nc.gpsimd.tensor_tensor(gf_col[:], gain_col[:], fringe_col[:], ALU.mult)
+        nc.vector.tensor_tensor(gf_col[:], gain_col[:], fringe_col[:], ALU.mult)
 
         tab_codes = [held([P, T], I32, "tab_codes%d" % a) for a in range(2)]
         nc.sync.dma_start(tab_codes[0][:], tab_words[0].rearrange("p t i -> p (t i)").bitcast(I32))
@@ -112,7 +112,7 @@ def tile_list_tyre_shear_features_kernel(
             d = held([P, PACK, HALF], F32, "damp%d%d" % (b, h))
             r = held([P, PACK, HALF], F32, "resp%d%d" % (b, h))
             for t in range(PACK):
-                bank = psum.tile([P, HALF], F32, name="by_bank", tag="by_bank", bufs=5)
+                bank = psum.tile([P, HALF], F32, name="by_bank", tag="by_bank", bufs=4)
                 nc.tensor.matmul_mx(
                     out=bank[:],
                     lhsT=w2_codes[b][:, 2 * P * t : 2 * P * (t + 1)].bitcast(FP4X4),
@@ -122,10 +122,16 @@ def tile_list_tyre_shear_features_kernel(
                     start=True,
                     stop=True,
                 )
+                on_vector = (b, h) == (0, 0) and t in (2, 3)
+                if on_vector:
+                    nc.vector.tensor_scalar(
+                        r[:, t, :], bank[:], fringe_col[:, b, t : t + 1], gain_col[:, b, t : t + 1], ALU.add, ALU.mult
+                    )
                 nc.scalar.activation(d[:, t, :], bank[:], ACT.Square, bias=fringe_col[:, b, t : t + 1])
-                nc.scalar.activation(
-                    r[:, t, :], bank[:], ACT.Identity, bias=gf_col[:, b, t : t + 1], scale=gain_col[:, b, t : t + 1]
-                )
+                if not on_vector:
+                    nc.scalar.activation(
+                        r[:, t, :], bank[:], ACT.Identity, bias=gf_col[:, b, t : t + 1], scale=gain_col[:, b, t : t + 1]
+                    )
                 if t % 2 == 1:
                     pair = d[:, t - 1 : t + 1, :]
                     nc.scalar.activation(pair, pair, ACT.Abs_reciprocal_sqrt, bias=1.0)
@@ -162,72 +168,100 @@ def tile_list_tyre_shear_features_kernel(
         w1_q, w3_q = {}, {}
 
         def prepare_w1(b):
-            grouped = [group_weight(w1_raw[b, a], False) for a in range(2)]
+            grouped = [group_weight(w1_raw[b, a], (b, a) in ((1, 1),)) for a in range(2)]
             for a in range(2):
                 w1_q[b, a] = quantise_weight(grouped[a], "w1_%d%d" % (b, a))
 
         z_q = {}
 
-        def casing_terms(b, h):
-            d, r = damp[b, h], resp[b, h]
-            for t in range(PACK):
-                bank = psum.tile([P, HALF], F32, name="a_bank", tag="a_bank", bufs=3)
-                for a in range(2):
-                    codes, plane = w1_q[b, a]
-                    nc.tensor.matmul_mx(
-                        out=bank[:],
-                        lhsT=codes[:, P * t : P * (t + 1)].bitcast(FP8X4),
-                        lhsT_scale=plane[:, P * t : P * (t + 1)],
-                        rhs=v_codes[a, h][:].bitcast(FP8X4),
-                        rhs_scale=v_plane[h][4 * a : P, :],
-                        start=(a == 0),
-                        stop=(a == 1),
-                    )
-                nc.vector.tensor_tensor(d[:, t, :], bank[:], d[:, t, :], ALU.mult)
-            grouped = []
-            for c in range(2):
-                cols = slice(CHUNK * c, CHUNK * (c + 1))
-                g = ring.tile([P, PACK * CHUNK], BF16, name="z_grouped", tag="z_grouped", bufs=4, align_bytes=64)
-                nc.vector.tensor_tensor(
-                    g[:].rearrange("p (c i t) -> p c t i", i=4, t=PACK),
-                    d[:, :, cols].rearrange("p t (c i) -> p c t i", i=4),
-                    r[:, :, cols].rearrange("p t (c i) -> p c t i", i=4),
-                    ALU.add,
+        def quantise_z(b, h, c, grouped):
+            codes = held([P, CHUNK], U32, "z_codes%d%d%d" % (b, h, c))
+            plane = held([P, CHUNK], U8, "z_plane%d%d%d" % (b, h, c))
+            nc.vector.quantize_mx(out=codes[:].bitcast(FP8X4), scales=plane[:], in_=grouped[:])
+            z_q[b, 2 * h + c] = (codes, plane)
+
+        def casing_bank(b, h, t):
+            bank = psum.tile([P, HALF], F32, name="a_bank", tag="a_bank", bufs=4)
+            for a in range(2):
+                codes, plane = w1_q[b, a]
+                nc.tensor.matmul_mx(
+                    out=bank[:],
+                    lhsT=codes[:, P * t : P * (t + 1)].bitcast(FP8X4),
+                    lhsT_scale=plane[:, P * t : P * (t + 1)],
+                    rhs=v_codes[a, h][:].bitcast(FP8X4),
+                    rhs_scale=v_plane[h][4 * a : P, :],
+                    start=(a == 0),
+                    stop=(a == 1),
                 )
-                grouped.append(g)
-            for c in range(2):
-                codes = held([P, CHUNK], U32, "z_codes%d%d%d" % (b, h, c))
-                plane = held([P, CHUNK], U8, "z_plane%d%d%d" % (b, h, c))
-                nc.vector.quantize_mx(out=codes[:].bitcast(FP8X4), scales=plane[:], in_=grouped[c][:])
-                z_q[b, 2 * h + c] = (codes, plane)
+            return bank
+
+        def sum_terms(b, h, c):
+            cols = slice(CHUNK * c, CHUNK * (c + 1))
+            g = ring.tile([P, PACK * CHUNK], BF16, name="z_grouped", tag="z_grouped", bufs=4, align_bytes=64)
+            nc.vector.tensor_tensor(
+                g[:].rearrange("p (c i t) -> p c t i", i=2, t=PACK),
+                damp[b, h][:, :, cols].rearrange("p t (c i) -> p c t i", i=2),
+                resp[b, h][:, :, cols].rearrange("p t (c i) -> p c t i", i=2),
+                ALU.add,
+            )
+            return g
+
+        def casing_terms(b, h, eager=False):
+            d = damp[b, h]
+            banks = [casing_bank(b, h, t) for t in range(PACK)]
+            if eager:
+                for c in range(2):
+                    cols = slice(CHUNK * c, CHUNK * (c + 1))
+                    for t in range(PACK):
+                        nc.vector.tensor_tensor(d[:, t, cols], banks[t][:, cols], d[:, t, cols], ALU.mult)
+                    quantise_z(b, h, c, sum_terms(b, h, c))
+            else:
+                for t in range(PACK):
+                    nc.vector.tensor_tensor(d[:, t, :], banks[t][:], d[:, t, :], ALU.mult)
+                grouped = [sum_terms(b, h, c) for c in range(2)]
+                for c in range(2):
+                    quantise_z(b, h, c, grouped[c])
 
         y_plane = held([P, S], U8, "y_plane")
         out_rows = out_0.rearrange("(p t) j -> p t j", t=PACK)
         out_words = out_1[0].rearrange("p m t -> p (m t)").bitcast(I32)
 
+        def feature_pass(out, c, t, b):
+            w_codes, w_plane = w3_q[b]
+            z_codes, z_plane = z_q[b, c]
+            nc.tensor.matmul_mx(
+                out=out,
+                lhsT=w_codes[:, P * t : P * (t + 1)].bitcast(FP8X4),
+                lhsT_scale=w_plane[:, P * t : P * (t + 1)],
+                rhs=z_codes[:].bitcast(FP8X4),
+                rhs_scale=z_plane[:],
+                start=(b == 0),
+                stop=(b == 1),
+            )
+
         def features(c):
-            cols = slice(CHUNK * c, CHUNK * (c + 1))
-            y = ring.tile([P, PACK, CHUNK], F32, name="y", tag="y", bufs=3, align_bytes=64)
-            for u in range(2):
-                bank = psum.tile([P, 2, CHUNK], F32, name="by_bank", tag="by_bank", bufs=5)
-                for e in range(2):
-                    t = 2 * u + e
-                    for b in range(2):
-                        w_codes, w_plane = w3_q[b]
-                        z_codes, z_plane = z_q[b, c]
-                        nc.tensor.matmul_mx(
-                            out=bank[:, e, :],
-                            lhsT=w_codes[:, P * t : P * (t + 1)].bitcast(FP8X4),
-                            lhsT_scale=w_plane[:, P * t : P * (t + 1)],
-                            rhs=z_codes[:].bitcast(FP8X4),
-                            rhs_scale=z_plane[:],
-                            start=(b == 0),
-                            stop=(b == 1),
-                        )
-                nc.scalar.copy(y[:, 2 * u : 2 * u + 2, :], bank[:])
-            nc.sync.dma_start(out_rows[:, :, cols], y[:])
-            g = ring.tile([P, PACK * CHUNK], BF16, name="y_grouped", tag="y_grouped", align_bytes=64)
-            copy = nc.scalar.copy if c < 2 else nc.vector.tensor_copy
+            y = ring.tile([P, PACK, CHUNK], F32, name="y", tag="y", bufs=4, align_bytes=64)
+            if c < 3:
+                for u in range(2):
+                    bank = psum.tile([P, 2, CHUNK], F32, name="by_bank", tag="by_bank", bufs=4)
+                    for e in range(2):
+                        for b in range(2):
+                            feature_pass(bank[:, e, :], c, 2 * u + e, b)
+                    nc.scalar.copy(y[:, 2 * u : 2 * u + 2, :], bank[:])
+            else:
+                banks = [psum.tile([P, CHUNK], F32, name="a_bank", tag="a_bank", bufs=4) for t in range(PACK)]
+                for b in range(2):
+                    for t in range(PACK):
+                        feature_pass(banks[t][:], c, t, b)
+                for t in range(PACK):
+                    copy = nc.vector.tensor_copy if t in (1, 3) else nc.scalar.copy
+                    copy(y[:, t, :], banks[t][:])
+            nc.sync.dma_start(out_rows[:, :, CHUNK * c : CHUNK * (c + 1)], y[:])
+            return y
+
+        def group_features(y, on_scalar):
+            g = ring.tile([P, PACK * CHUNK], BF16, name="y_grouped", tag="y_grouped", bufs=4, align_bytes=64)
+            copy = nc.scalar.copy if on_scalar else nc.vector.tensor_copy
             copy(
                 g[:].rearrange("p (c i t) -> p c t i", i=4, t=PACK),
                 y[:].rearrange("p t (c i) -> p c t i", i=4),
@@ -243,25 +277,26 @@ def tile_list_tyre_shear_features_kernel(
         frame_terms(0, 0)
         gather(0)
         prepare_w1(0)
-        frame_terms(1, 0)
+        frame_terms(0, 1)
         gather(1)
         casing_terms(0, 0)
         prepare_w1(1)
-        frame_terms(0, 1)
-        casing_terms(1, 0)
+        frame_terms(1, 0)
+        casing_terms(0, 1)
         w3_grouped = [group_weight(w3_raw[b], True) for b in range(2)]
         frame_terms(1, 1)
-        casing_terms(0, 1)
+        casing_terms(1, 0)
         for b in range(2):
             w3_q[b] = quantise_weight(w3_grouped[b], "w3_%d" % b)
-        first = [features(c) for c in range(2)]
-        casing_terms(1, 1)
+        first = [group_features(features(c), True) for c in range(2)]
+        casing_terms(1, 1, eager=True)
+        last = [features(c) for c in range(2, 4)]
         for c in range(2):
             planes(c, first[c])
-        last = [features(c) for c in range(2, 4)]
         for c in range(2, 4):
-            planes(c, last[c - 2])
+            planes(c, group_features(last[c - 2], False))
         for q in range(4):
-            nc.sync.dma_start(
+            queue = nc.sync if q % 2 == 0 else nc.scalar
+            queue.dma_start(
                 out_2[0, 4 * q : 4 * q + 4, :].bitcast(I32), y_plane[32 * q : 32 * q + 4, :].bitcast(I32)
             )

@@ -21,6 +21,7 @@ PACK = 4
 PASS = P * PACK
 HALF = 512
 CHUNK = 256
+CHUNKS = ((0, 256), (256, 256), (512, 256), (768, 256))
 
 
 def tile_list_tyre_shear_features_kernel(
@@ -41,6 +42,8 @@ def tile_list_tyre_shear_features_kernel(
         w2_plane = held([P, H], U8, "w2_plane")
         xs_plane = held([P, S], U8, "xs_plane")
         tab_plane = held([P, T], U8, "tab_plane")
+        nc.vector.memset(w2_plane[:].bitcast(I32), 0)
+        nc.gpsimd.memset(xs_plane[:].bitcast(I32), 0)
         nc.vector.memset(tab_plane[:].bitcast(I32), 0)
 
         warm_in = held([P, 1], F32, "warm_in")
@@ -51,21 +54,20 @@ def tile_list_tyre_shear_features_kernel(
         w2_raw = held([P, 2 * H], U8, "w2_raw")
         def load_quadrant(queue, plane, scales, q):
             rows = scales[0, 4 * q : 4 * q + 4, :].bitcast(I32)
-            queue.dma_start(
-                plane[32 * q : 32 * q + 32, :].bitcast(I32), rows.unsqueeze(0).broadcast_to([8, 4, rows.shape[1]])
-            )
+            queue.dma_start(plane[32 * q : 32 * q + 4, :].bitcast(I32), rows)
 
         for q in range(4):
             load_quadrant(nc.sync, w2_plane, w2_scales, q)
         nc.sync.dma_start(w2_raw[:].bitcast(I32), w2_words[0].bitcast(I32))
-        xs_codes = held([P, S], I32, "xs_codes")
-        nc.sync.dma_start(xs_codes[:], xs_words[0].rearrange("p c i -> p (c i)").bitcast(I32))
+        xs_codes = [held([P, HALF], I32, "xs_codes%d" % h) for h in range(2)]
+        xs_rows = xs_words[0].rearrange("p c i -> p (c i)").bitcast(I32)
+        nc.sync.dma_start(xs_codes[0][:], xs_rows[:, 0:HALF])
         fringe_col = held([P, 2, PACK], F32, "fringe_col")
         gain_col = held([P, 2, PACK], F32, "gain_col")
         gf_col = held([P, 2, PACK], F32, "gf_col")
         for q in range(4):
-            load_quadrant(nc.sync, xs_plane, xs_scales, q)
-        nc.gpsimd.dma_start(fringe_col[:], fringe.rearrange("(b p t) -> p b t", b=2, t=PACK))
+            load_quadrant(nc.gpsimd if q == 3 else nc.sync, xs_plane, xs_scales, q)
+        nc.sync.dma_start(fringe_col[:], fringe.rearrange("(b p t) -> p b t", b=2, t=PACK))
         nc.sync.dma_start(gain_col[:], gain.rearrange("(b p t) -> p b t", b=2, t=PACK))
         nc.vector.tensor_tensor(gf_col[:], gain_col[:], fringe_col[:], ALU.mult)
 
@@ -78,6 +80,7 @@ def tile_list_tyre_shear_features_kernel(
             )
         nc.sync.dma_start(tab_codes[1][:], tab_words[1].rearrange("p t i -> p (t i)").bitcast(I32))
 
+        nc.sync.dma_start(xs_codes[1][:], xs_rows[:, HALF:S])
         w1_raw = {}
         for b in range(2):
             for a in range(2):
@@ -117,12 +120,12 @@ def tile_list_tyre_shear_features_kernel(
                     out=bank[:],
                     lhsT=w2_codes[b][:, 2 * P * t : 2 * P * (t + 1)].bitcast(FP4X4),
                     lhsT_scale=w2_dealt[b][:, P * t : P * (t + 1)],
-                    rhs=xs_codes[:, cols].bitcast(FP8X4),
+                    rhs=xs_codes[h][:].bitcast(FP8X4),
                     rhs_scale=xs_plane[:, cols],
                     start=True,
                     stop=True,
                 )
-                on_vector = (b, h) == (0, 0) and t in (2, 3)
+                on_vector = (b, h) == (0, 0) and t in (1, 2, 3)
                 if on_vector:
                     nc.vector.tensor_scalar(
                         r[:, t, :], bank[:], fringe_col[:, b, t : t + 1], gain_col[:, b, t : t + 1], ALU.add, ALU.mult
@@ -132,9 +135,10 @@ def tile_list_tyre_shear_features_kernel(
                     nc.scalar.activation(
                         r[:, t, :], bank[:], ACT.Identity, bias=gf_col[:, b, t : t + 1], scale=gain_col[:, b, t : t + 1]
                     )
-                if t % 2 == 1:
-                    pair = d[:, t - 1 : t + 1, :]
-                    nc.scalar.activation(pair, pair, ACT.Abs_reciprocal_sqrt, bias=1.0)
+                span = 2 if (b, h) == (1, 1) else PACK
+                if (t + 1) % span == 0:
+                    part = d[:, t + 1 - span : t + 1, :]
+                    nc.scalar.activation(part, part, ACT.Abs_reciprocal_sqrt, bias=1.0)
             damp[b, h], resp[b, h] = d, r
 
         v_codes, v_plane = {}, {}
@@ -153,10 +157,9 @@ def tile_list_tyre_shear_features_kernel(
             grouped = ring.tile([P, PACK * PASS], BF16, name="w_grouped", tag="w_grouped", bufs=4, align_bytes=64)
             dst = grouped[:].rearrange("p (t q j) -> p q j t", t=PACK, j=PACK)
             src = raw[:].rearrange("p j (q t) -> p q j t", t=PACK)
-            if on_scalar:
-                nc.scalar.copy(dst, src)
-            else:
-                nc.vector.tensor_copy(dst, src)
+            copy = nc.scalar.copy if on_scalar else nc.vector.tensor_copy
+            for t in range(0, PACK, 2):
+                copy(dst[:, :, :, t : t + 2], src[:, :, :, t : t + 2])
             return grouped
 
         def quantise_weight(grouped, name):
@@ -175,10 +178,11 @@ def tile_list_tyre_shear_features_kernel(
         z_q = {}
 
         def quantise_z(b, h, c, grouped):
-            codes = held([P, CHUNK], U32, "z_codes%d%d%d" % (b, h, c))
-            plane = held([P, CHUNK], U8, "z_plane%d%d%d" % (b, h, c))
+            width = CHUNKS[c][1]
+            codes = held([P, width], U32, "z_codes%d%d" % (b, c))
+            plane = held([P, width], U8, "z_plane%d%d" % (b, c))
             nc.vector.quantize_mx(out=codes[:].bitcast(FP8X4), scales=plane[:], in_=grouped[:])
-            z_q[b, 2 * h + c] = (codes, plane)
+            z_q[b, c] = (codes, plane)
 
         def casing_bank(b, h, t):
             bank = psum.tile([P, HALF], F32, name="a_bank", tag="a_bank", bufs=4)
@@ -196,8 +200,9 @@ def tile_list_tyre_shear_features_kernel(
             return bank
 
         def sum_terms(b, h, c):
-            cols = slice(CHUNK * c, CHUNK * (c + 1))
-            g = ring.tile([P, PACK * CHUNK], BF16, name="z_grouped", tag="z_grouped", bufs=4, align_bytes=64)
+            start, width = CHUNKS[c]
+            cols = slice(start - HALF * h, start - HALF * h + width)
+            g = ring.tile([P, PACK * width], BF16, name="z_grouped", tag="z_grouped", bufs=4, align_bytes=64)
             nc.vector.tensor_tensor(
                 g[:].rearrange("p (c i t) -> p c t i", i=2, t=PACK),
                 damp[b, h][:, :, cols].rearrange("p t (c i) -> p c t i", i=2),
@@ -209,18 +214,20 @@ def tile_list_tyre_shear_features_kernel(
         def casing_terms(b, h, eager=False):
             d = damp[b, h]
             banks = [casing_bank(b, h, t) for t in range(PACK)]
+            mine = [c for c in range(len(CHUNKS)) if CHUNKS[c][0] // HALF == h]
             if eager:
-                for c in range(2):
-                    cols = slice(CHUNK * c, CHUNK * (c + 1))
+                for c in mine:
+                    start, width = CHUNKS[c]
+                    cols = slice(start - HALF * h, start - HALF * h + width)
                     for t in range(PACK):
                         nc.vector.tensor_tensor(d[:, t, cols], banks[t][:, cols], d[:, t, cols], ALU.mult)
                     quantise_z(b, h, c, sum_terms(b, h, c))
             else:
                 for t in range(PACK):
                     nc.vector.tensor_tensor(d[:, t, :], banks[t][:], d[:, t, :], ALU.mult)
-                grouped = [sum_terms(b, h, c) for c in range(2)]
-                for c in range(2):
-                    quantise_z(b, h, c, grouped[c])
+                grouped = [sum_terms(b, h, c) for c in mine]
+                for c, g in zip(mine, grouped):
+                    quantise_z(b, h, c, g)
 
         y_plane = held([P, S], U8, "y_plane")
         out_rows = out_0.rearrange("(p t) j -> p t j", t=PACK)
@@ -240,28 +247,31 @@ def tile_list_tyre_shear_features_kernel(
             )
 
         def features(c):
-            y = ring.tile([P, PACK, CHUNK], F32, name="y", tag="y", bufs=4, align_bytes=64)
-            if c < 3:
-                for u in range(2):
-                    bank = psum.tile([P, 2, CHUNK], F32, name="by_bank", tag="by_bank", bufs=4)
-                    for e in range(2):
+            start, width = CHUNKS[c]
+            y = ring.tile([P, PACK, width], F32, name="y", tag="y", bufs=4, align_bytes=64)
+            if c not in (3,):
+                side = HALF // width
+                for u in range(PACK // side):
+                    bank = psum.tile([P, side, width], F32, name="by_bank", tag="by_bank", bufs=4)
+                    for e in range(side):
                         for b in range(2):
-                            feature_pass(bank[:, e, :], c, 2 * u + e, b)
-                    nc.scalar.copy(y[:, 2 * u : 2 * u + 2, :], bank[:])
+                            feature_pass(bank[:, e, :], c, side * u + e, b)
+                    copy = nc.vector.tensor_copy if (c, u) in () else nc.scalar.copy
+                    copy(y[:, side * u : side * (u + 1), :], bank[:])
             else:
-                banks = [psum.tile([P, CHUNK], F32, name="a_bank", tag="a_bank", bufs=4) for t in range(PACK)]
+                banks = [psum.tile([P, width], F32, name="a_bank", tag="a_bank", bufs=4) for t in range(PACK)]
                 for b in range(2):
                     for t in range(PACK):
                         feature_pass(banks[t][:], c, t, b)
                 for t in range(PACK):
                     copy = nc.vector.tensor_copy if t in (1, 3) else nc.scalar.copy
                     copy(y[:, t, :], banks[t][:])
-            nc.sync.dma_start(out_rows[:, :, CHUNK * c : CHUNK * (c + 1)], y[:])
+            nc.sync.dma_start(out_rows[:, :, start : start + width], y[:])
             return y
 
-        def group_features(y, on_scalar):
-            g = ring.tile([P, PACK * CHUNK], BF16, name="y_grouped", tag="y_grouped", bufs=4, align_bytes=64)
-            copy = nc.scalar.copy if on_scalar else nc.vector.tensor_copy
+        def group_features(c, y):
+            g = ring.tile([P, PACK * CHUNKS[c][1]], BF16, name="y_grouped", tag="y_grouped", bufs=4, align_bytes=64)
+            copy = nc.scalar.copy if c in (0, 1, 2) else nc.vector.tensor_copy
             copy(
                 g[:].rearrange("p (c i t) -> p c t i", i=4, t=PACK),
                 y[:].rearrange("p t (c i) -> p c t i", i=4),
@@ -269,8 +279,9 @@ def tile_list_tyre_shear_features_kernel(
             return g
 
         def planes(c, g):
-            cols = slice(CHUNK * c, CHUNK * (c + 1))
-            codes = held([P, CHUNK], U32, "y_codes%d" % c)
+            start, width = CHUNKS[c]
+            cols = slice(start, start + width)
+            codes = held([P, width], U32, "y_codes%d" % c)
             nc.vector.quantize_mx(out=codes[:].bitcast(FP8X4), scales=y_plane[:, cols], in_=g[:])
             nc.sync.dma_start(out_words[:, cols], codes[:].bitcast(I32))
 
@@ -280,21 +291,21 @@ def tile_list_tyre_shear_features_kernel(
         frame_terms(0, 1)
         gather(1)
         casing_terms(0, 0)
-        prepare_w1(1)
         frame_terms(1, 0)
+        prepare_w1(1)
         casing_terms(0, 1)
         w3_grouped = [group_weight(w3_raw[b], True) for b in range(2)]
         frame_terms(1, 1)
         casing_terms(1, 0)
         for b in range(2):
             w3_q[b] = quantise_weight(w3_grouped[b], "w3_%d" % b)
-        first = [group_features(features(c), True) for c in range(2)]
+        first = [group_features(c, features(c)) for c in range(2)]
         casing_terms(1, 1, eager=True)
-        last = [features(c) for c in range(2, 4)]
+        last = [features(c) for c in range(2, len(CHUNKS))]
         for c in range(2):
             planes(c, first[c])
-        for c in range(2, 4):
-            planes(c, group_features(last[c - 2], False))
+        for c in range(2, len(CHUNKS)):
+            planes(c, group_features(c, last[c - 2]))
         for q in range(4):
             queue = nc.sync if q % 2 == 0 else nc.scalar
             queue.dma_start(

@@ -19,9 +19,14 @@ ALU = mybir.AluOpType
 P = 128
 PACK = 4
 PASS = P * PACK
-HALF = 512
-CHUNK = 256
-CHUNKS = ((0, 256), (256, 256), (512, 256), (768, 256))
+QUADS = 4
+HALF = S // 2
+CHUNK = HALF // 2
+CHUNKS = S // CHUNK
+BANKS = 4
+LAST_UNIT = (1, 1)
+EARLY_ON_VECTOR = 3
+W1_ON_SCALAR = (1, 1)
 
 
 def tile_list_tyre_shear_features_kernel(
@@ -51,36 +56,37 @@ def tile_list_tyre_shear_features_kernel(
         nc.vector.memset(warm_in[:], 1.0)
         nc.scalar.activation(warm_out[:], warm_in[:], ACT.Abs_reciprocal_sqrt)
 
-        w2_raw = held([P, 2 * H], U8, "w2_raw")
-        def load_quadrant(queue, plane, scales, q):
-            rows = scales[0, 4 * q : 4 * q + 4, :].bitcast(I32)
-            queue.dma_start(plane[32 * q : 32 * q + 4, :].bitcast(I32), rows)
+        def load_quadrant(queue, plane, scales, quad):
+            rows = scales[0, 4 * quad : 4 * quad + 4, :].bitcast(I32)
+            queue.dma_start(plane[32 * quad : 32 * quad + 4, :].bitcast(I32), rows)
 
-        for q in range(4):
-            load_quadrant(nc.sync, w2_plane, w2_scales, q)
+        for quad in range(QUADS):
+            load_quadrant(nc.sync, w2_plane, w2_scales, quad)
+        w2_raw = held([P, 2 * H], U8, "w2_raw")
         nc.sync.dma_start(w2_raw[:].bitcast(I32), w2_words[0].bitcast(I32))
         xs_codes = [held([P, HALF], I32, "xs_codes%d" % h) for h in range(2)]
         xs_rows = xs_words[0].rearrange("p c i -> p (c i)").bitcast(I32)
         nc.sync.dma_start(xs_codes[0][:], xs_rows[:, 0:HALF])
+        for quad in range(QUADS):
+            load_quadrant(nc.gpsimd if quad == QUADS - 1 else nc.sync, xs_plane, xs_scales, quad)
         fringe_col = held([P, 2, PACK], F32, "fringe_col")
         gain_col = held([P, 2, PACK], F32, "gain_col")
-        gf_col = held([P, 2, PACK], F32, "gf_col")
-        for q in range(4):
-            load_quadrant(nc.gpsimd if q == 3 else nc.sync, xs_plane, xs_scales, q)
+        gain_fringe = held([P, 2, PACK], F32, "gain_fringe")
         nc.sync.dma_start(fringe_col[:], fringe.rearrange("(b p t) -> p b t", b=2, t=PACK))
         nc.sync.dma_start(gain_col[:], gain.rearrange("(b p t) -> p b t", b=2, t=PACK))
-        nc.vector.tensor_tensor(gf_col[:], gain_col[:], fringe_col[:], ALU.mult)
+        nc.vector.tensor_tensor(gain_fringe[:], gain_col[:], fringe_col[:], ALU.mult)
 
         tab_codes = [held([P, T], I32, "tab_codes%d" % a) for a in range(2)]
         nc.sync.dma_start(tab_codes[0][:], tab_words[0].rearrange("p t i -> p (t i)").bitcast(I32))
         nc.sync.dma_start(offsets[:], offs)
-        for q in range(4):
-            nc.sync.dma_start(
-                tab_plane[32 * q : 32 * q + 8, :].bitcast(I32), tab_scales[:, 4 * q : 4 * q + 4, :].bitcast(I32)
+        for quad in range(QUADS):
+            nc.gpsimd.dma_start(
+                tab_plane[32 * quad : 32 * quad + 8, :].bitcast(I32),
+                tab_scales[:, 4 * quad : 4 * quad + 4, :].bitcast(I32),
             )
         nc.sync.dma_start(tab_codes[1][:], tab_words[1].rearrange("p t i -> p (t i)").bitcast(I32))
-
         nc.sync.dma_start(xs_codes[1][:], xs_rows[:, HALF:S])
+
         w1_raw = {}
         for b in range(2):
             for a in range(2):
@@ -97,15 +103,14 @@ def tile_list_tyre_shear_features_kernel(
         w2_codes, w2_dealt = {}, {}
         for b in range(2):
             codes = held([P, 2 * PASS], U8, "w2_codes%d" % b)
-            nc.vector.tensor_copy(
-                codes[:].rearrange("p (t q e) -> p q t e", t=PACK, e=2),
-                w2_raw[:, 2 * PASS * b : 2 * PASS * (b + 1)].rearrange("p (q t e) -> p q t e", t=PACK, e=2),
-            )
             plane = held([P, PASS], U8, "w2_dealt%d" % b)
-            nc.vector.tensor_copy(
-                plane[:].rearrange("p (t q) -> p q t", t=PACK),
-                w2_plane[:, PASS * b : PASS * (b + 1)].rearrange("p (q t) -> p q t", t=PACK),
-            )
+            code_dst = codes[:].rearrange("p (t q e) -> p q t e", t=PACK, e=2)
+            code_src = w2_raw[:, 2 * PASS * b : 2 * PASS * (b + 1)].rearrange("p (q t e) -> p q t e", t=PACK, e=2)
+            plane_dst = plane[:].rearrange("p (t q) -> p q t", t=PACK)
+            plane_src = w2_plane[:, PASS * b : PASS * (b + 1)].rearrange("p (q t) -> p q t", t=PACK)
+            for t in range(0, PACK, 2):
+                nc.vector.tensor_copy(code_dst[:, :, t : t + 2, :], code_src[:, :, t : t + 2, :])
+                nc.vector.tensor_copy(plane_dst[:, :, t : t + 2], plane_src[:, :, t : t + 2])
             w2_codes[b], w2_dealt[b] = codes, plane
 
         damp, resp = {}, {}
@@ -114,8 +119,9 @@ def tile_list_tyre_shear_features_kernel(
             cols = slice(HALF * h, HALF * (h + 1))
             d = held([P, PACK, HALF], F32, "damp%d%d" % (b, h))
             r = held([P, PACK, HALF], F32, "resp%d%d" % (b, h))
+            span = 2 if (b, h) == LAST_UNIT else PACK
             for t in range(PACK):
-                bank = psum.tile([P, HALF], F32, name="by_bank", tag="by_bank", bufs=4)
+                bank = psum.tile([P, HALF], F32, name="frame_bank", tag="frame_bank", bufs=BANKS)
                 nc.tensor.matmul_mx(
                     out=bank[:],
                     lhsT=w2_codes[b][:, 2 * P * t : 2 * P * (t + 1)].bitcast(FP4X4),
@@ -125,33 +131,27 @@ def tile_list_tyre_shear_features_kernel(
                     start=True,
                     stop=True,
                 )
-                on_vector = (b, h) == (0, 0) and t in (1, 2, 3)
+                offset, factor = fringe_col[:, b, t : t + 1], gain_col[:, b, t : t + 1]
+                on_vector = (b, h) == (0, 0) and t >= PACK - EARLY_ON_VECTOR
                 if on_vector:
-                    nc.vector.tensor_scalar(
-                        r[:, t, :], bank[:], fringe_col[:, b, t : t + 1], gain_col[:, b, t : t + 1], ALU.add, ALU.mult
-                    )
-                nc.scalar.activation(d[:, t, :], bank[:], ACT.Square, bias=fringe_col[:, b, t : t + 1])
+                    nc.vector.tensor_scalar(r[:, t, :], bank[:], offset, factor, ALU.add, ALU.mult)
+                nc.scalar.activation(d[:, t, :], bank[:], ACT.Square, bias=offset)
                 if not on_vector:
                     nc.scalar.activation(
-                        r[:, t, :], bank[:], ACT.Identity, bias=gf_col[:, b, t : t + 1], scale=gain_col[:, b, t : t + 1]
+                        r[:, t, :], bank[:], ACT.Identity, bias=gain_fringe[:, b, t : t + 1], scale=factor
                     )
-                span = 2 if (b, h) == (1, 1) else PACK
                 if (t + 1) % span == 0:
                     part = d[:, t + 1 - span : t + 1, :]
                     nc.scalar.activation(part, part, ACT.Abs_reciprocal_sqrt, bias=1.0)
             damp[b, h], resp[b, h] = d, r
 
-        v_codes, v_plane = {}, {}
-
-        def gather(h):
-            picked = offsets[:, (HALF // 16) * h : (HALF // 16) * (h + 1)]
+        def gather():
+            codes = [held([P, S], U32, "v_codes%d" % a) for a in range(2)]
             for a in range(2):
-                codes = held([P, HALF], U32, "v_codes%d%d" % (a, h))
-                nc.vector.tensor_copy(codes[:], tab_codes[a][:].bitcast(U32).indirect(picked))
-                v_codes[a, h] = codes
-            plane = held([P, HALF], U8, "v_plane%d" % h)
-            nc.vector.tensor_copy(plane[:], tab_plane[:].indirect(picked))
-            v_plane[h] = plane
+                nc.vector.tensor_copy(codes[a][:], tab_codes[a][:].bitcast(U32).indirect(offsets[:]))
+            plane = held([P, S], U8, "v_plane")
+            nc.vector.tensor_copy(plane[:], tab_plane[:].indirect(offsets[:]))
+            return codes, plane
 
         def group_weight(raw, on_scalar):
             grouped = ring.tile([P, PACK * PASS], BF16, name="w_grouped", tag="w_grouped", bufs=4, align_bytes=64)
@@ -162,134 +162,116 @@ def tile_list_tyre_shear_features_kernel(
                 copy(dst[:, :, :, t : t + 2], src[:, :, :, t : t + 2])
             return grouped
 
-        def quantise_weight(grouped, name):
-            codes = held([P, PASS], U32, name + "_codes")
-            plane = held([P, PASS], U8, name + "_plane")
+        def quantise(grouped, width, name):
+            codes = held([P, width], U32, name + "_codes")
+            plane = held([P, width], U8, name + "_plane")
             nc.vector.quantize_mx(out=codes[:].bitcast(FP8X4), scales=plane[:], in_=grouped[:])
             return codes, plane
 
-        w1_q, w3_q = {}, {}
+        w1_q, w3_q, z_q = {}, {}, {}
 
         def prepare_w1(b):
-            grouped = [group_weight(w1_raw[b, a], (b, a) in ((1, 1),)) for a in range(2)]
+            grouped = [group_weight(w1_raw[b, a], (b, a) == W1_ON_SCALAR) for a in range(2)]
             for a in range(2):
-                w1_q[b, a] = quantise_weight(grouped[a], "w1_%d%d" % (b, a))
-
-        z_q = {}
-
-        def quantise_z(b, h, c, grouped):
-            width = CHUNKS[c][1]
-            codes = held([P, width], U32, "z_codes%d%d" % (b, c))
-            plane = held([P, width], U8, "z_plane%d%d" % (b, c))
-            nc.vector.quantize_mx(out=codes[:].bitcast(FP8X4), scales=plane[:], in_=grouped[:])
-            z_q[b, c] = (codes, plane)
+                w1_q[b, a] = quantise(grouped[a], PASS, "w1_%d%d" % (b, a))
 
         def casing_bank(b, h, t):
-            bank = psum.tile([P, HALF], F32, name="a_bank", tag="a_bank", bufs=4)
+            cols = slice(HALF * h, HALF * (h + 1))
+            bank = psum.tile([P, HALF], F32, name="casing_bank", tag="casing_bank", bufs=BANKS)
             for a in range(2):
                 codes, plane = w1_q[b, a]
                 nc.tensor.matmul_mx(
                     out=bank[:],
                     lhsT=codes[:, P * t : P * (t + 1)].bitcast(FP8X4),
                     lhsT_scale=plane[:, P * t : P * (t + 1)],
-                    rhs=v_codes[a, h][:].bitcast(FP8X4),
-                    rhs_scale=v_plane[h][4 * a : P, :],
+                    rhs=v_codes[a][:, cols].bitcast(FP8X4),
+                    rhs_scale=v_plane[4 * a : P, cols],
                     start=(a == 0),
                     stop=(a == 1),
                 )
             return bank
 
-        def sum_terms(b, h, c):
-            start, width = CHUNKS[c]
-            cols = slice(start - HALF * h, start - HALF * h + width)
-            g = ring.tile([P, PACK * width], BF16, name="z_grouped", tag="z_grouped", bufs=4, align_bytes=64)
+        def finish_z(b, h, banks, start, width):
+            cols = slice(start, start + width)
+            d, r = damp[b, h], resp[b, h]
+            for t in range(PACK):
+                nc.vector.tensor_tensor(d[:, t, cols], banks[t][:, cols], d[:, t, cols], ALU.mult)
+            grouped = ring.tile([P, PACK * width], BF16, name="z_grouped", tag="z_grouped", bufs=3, align_bytes=64)
             nc.vector.tensor_tensor(
-                g[:].rearrange("p (c i t) -> p c t i", i=2, t=PACK),
-                damp[b, h][:, :, cols].rearrange("p t (c i) -> p c t i", i=2),
-                resp[b, h][:, :, cols].rearrange("p t (c i) -> p c t i", i=2),
+                grouped[:].rearrange("p (c i t) -> p c t i", i=2, t=PACK),
+                d[:, :, cols].rearrange("p t (c i) -> p c t i", i=2),
+                r[:, :, cols].rearrange("p t (c i) -> p c t i", i=2),
                 ALU.add,
             )
-            return g
+            codes, plane = quantise(grouped, width, "z_%d%d_%d" % (b, h, start))
+            for first in range(0, width, CHUNK):
+                chunk = (HALF * h + start + first) // CHUNK
+                z_q[b, chunk] = (codes[:, first : first + CHUNK], plane[:, first : first + CHUNK])
 
-        def casing_terms(b, h, eager=False):
-            d = damp[b, h]
+        def casing_terms(b, h):
             banks = [casing_bank(b, h, t) for t in range(PACK)]
-            mine = [c for c in range(len(CHUNKS)) if CHUNKS[c][0] // HALF == h]
-            if eager:
-                for c in mine:
-                    start, width = CHUNKS[c]
-                    cols = slice(start - HALF * h, start - HALF * h + width)
-                    for t in range(PACK):
-                        nc.vector.tensor_tensor(d[:, t, cols], banks[t][:, cols], d[:, t, cols], ALU.mult)
-                    quantise_z(b, h, c, sum_terms(b, h, c))
-            else:
-                for t in range(PACK):
-                    nc.vector.tensor_tensor(d[:, t, :], banks[t][:], d[:, t, :], ALU.mult)
-                grouped = [sum_terms(b, h, c) for c in mine]
-                for c, g in zip(mine, grouped):
-                    quantise_z(b, h, c, g)
+            width = CHUNK if (b, h) == LAST_UNIT else HALF
+            for start in range(0, HALF, width):
+                finish_z(b, h, banks, start, width)
 
         y_plane = held([P, S], U8, "y_plane")
         out_rows = out_0.rearrange("(p t) j -> p t j", t=PACK)
         out_words = out_1[0].rearrange("p m t -> p (m t)").bitcast(I32)
 
-        def feature_pass(out, c, t, b):
+        def feature_pass(out, chunk, t, b):
             w_codes, w_plane = w3_q[b]
-            z_codes, z_plane = z_q[b, c]
+            z_codes, z_plane = z_q[b, chunk]
             nc.tensor.matmul_mx(
                 out=out,
                 lhsT=w_codes[:, P * t : P * (t + 1)].bitcast(FP8X4),
                 lhsT_scale=w_plane[:, P * t : P * (t + 1)],
-                rhs=z_codes[:].bitcast(FP8X4),
-                rhs_scale=z_plane[:],
+                rhs=z_codes.bitcast(FP8X4),
+                rhs_scale=z_plane,
                 start=(b == 0),
                 stop=(b == 1),
             )
 
-        def features(c):
-            start, width = CHUNKS[c]
-            y = ring.tile([P, PACK, width], F32, name="y", tag="y", bufs=4, align_bytes=64)
-            if c not in (3,):
-                side = HALF // width
-                for u in range(PACK // side):
-                    bank = psum.tile([P, side, width], F32, name="by_bank", tag="by_bank", bufs=4)
-                    for e in range(side):
+        def features(chunk):
+            y = ring.tile([P, PACK, CHUNK], F32, name="y", tag="y", bufs=CHUNKS, align_bytes=64)
+            if chunk < CHUNKS - 1:
+                for u in range(0, PACK, 2):
+                    bank = psum.tile([P, 2, CHUNK], F32, name="frame_bank", tag="frame_bank", bufs=BANKS)
+                    for e in range(2):
                         for b in range(2):
-                            feature_pass(bank[:, e, :], c, side * u + e, b)
-                    copy = nc.vector.tensor_copy if (c, u) in () else nc.scalar.copy
-                    copy(y[:, side * u : side * (u + 1), :], bank[:])
+                            feature_pass(bank[:, e, :], chunk, u + e, b)
+                    nc.scalar.copy(y[:, u : u + 2, :], bank[:])
             else:
-                banks = [psum.tile([P, width], F32, name="a_bank", tag="a_bank", bufs=4) for t in range(PACK)]
+                banks = [
+                    psum.tile([P, CHUNK], F32, name="casing_bank", tag="casing_bank", bufs=BANKS) for t in range(PACK)
+                ]
                 for b in range(2):
                     for t in range(PACK):
-                        feature_pass(banks[t][:], c, t, b)
+                        feature_pass(banks[t][:], chunk, t, b)
                 for t in range(PACK):
-                    copy = nc.vector.tensor_copy if t in (1, 3) else nc.scalar.copy
+                    copy = nc.vector.tensor_copy if t % 2 == 1 else nc.scalar.copy
                     copy(y[:, t, :], banks[t][:])
-            nc.sync.dma_start(out_rows[:, :, start : start + width], y[:])
+            nc.sync.dma_start(out_rows[:, :, CHUNK * chunk : CHUNK * (chunk + 1)], y[:])
             return y
 
-        def group_features(c, y):
-            g = ring.tile([P, PACK * CHUNKS[c][1]], BF16, name="y_grouped", tag="y_grouped", bufs=4, align_bytes=64)
-            copy = nc.scalar.copy if c in (0, 1, 2) else nc.vector.tensor_copy
+        def group_features(chunk, y):
+            grouped = ring.tile([P, PACK * CHUNK], BF16, name="y_grouped", tag="y_grouped", bufs=CHUNKS, align_bytes=64)
+            copy = nc.scalar.copy if chunk < CHUNKS - 1 else nc.vector.tensor_copy
             copy(
-                g[:].rearrange("p (c i t) -> p c t i", i=4, t=PACK),
+                grouped[:].rearrange("p (c i t) -> p c t i", i=4, t=PACK),
                 y[:].rearrange("p t (c i) -> p c t i", i=4),
             )
-            return g
+            return grouped
 
-        def planes(c, g):
-            start, width = CHUNKS[c]
-            cols = slice(start, start + width)
-            codes = held([P, width], U32, "y_codes%d" % c)
-            nc.vector.quantize_mx(out=codes[:].bitcast(FP8X4), scales=y_plane[:, cols], in_=g[:])
+        def feature_planes(chunk, grouped):
+            cols = slice(CHUNK * chunk, CHUNK * (chunk + 1))
+            codes = held([P, CHUNK], U32, "y_codes%d" % chunk)
+            nc.vector.quantize_mx(out=codes[:].bitcast(FP8X4), scales=y_plane[:, cols], in_=grouped[:])
             nc.sync.dma_start(out_words[:, cols], codes[:].bitcast(I32))
 
         frame_terms(0, 0)
-        gather(0)
+        v_codes, v_plane = gather()
         prepare_w1(0)
         frame_terms(0, 1)
-        gather(1)
         casing_terms(0, 0)
         frame_terms(1, 0)
         prepare_w1(1)
@@ -298,16 +280,17 @@ def tile_list_tyre_shear_features_kernel(
         frame_terms(1, 1)
         casing_terms(1, 0)
         for b in range(2):
-            w3_q[b] = quantise_weight(w3_grouped[b], "w3_%d" % b)
-        first = [group_features(c, features(c)) for c in range(2)]
-        casing_terms(1, 1, eager=True)
-        last = [features(c) for c in range(2, len(CHUNKS))]
-        for c in range(2):
-            planes(c, first[c])
-        for c in range(2, len(CHUNKS)):
-            planes(c, group_features(c, last[c - 2]))
-        for q in range(4):
-            queue = nc.sync if q % 2 == 0 else nc.scalar
+            w3_q[b] = quantise(w3_grouped[b], N, "w3_%d" % b)
+        first_half = [group_features(chunk, features(chunk)) for chunk in range(CHUNKS // 2)]
+        casing_terms(1, 1)
+        second_half = [features(chunk) for chunk in range(CHUNKS // 2, CHUNKS)]
+        for chunk in range(CHUNKS // 2):
+            feature_planes(chunk, first_half[chunk])
+        for chunk in range(CHUNKS // 2, CHUNKS):
+            feature_planes(chunk, group_features(chunk, second_half[chunk - CHUNKS // 2]))
+        for quad in range(QUADS):
+            queue = nc.sync if quad % 2 == 0 else nc.scalar
             queue.dma_start(
-                out_2[0, 4 * q : 4 * q + 4, :].bitcast(I32), y_plane[32 * q : 32 * q + 4, :].bitcast(I32)
+                out_2[0, 4 * quad : 4 * quad + 4, :].bitcast(I32),
+                y_plane[32 * quad : 32 * quad + 4, :].bitcast(I32),
             )

@@ -25,7 +25,7 @@ CHUNK = HALF // 2
 CHUNKS = S // CHUNK
 BANKS = 4
 LAST_UNIT = (1, 1)
-EARLY_ON_VECTOR = 3
+FIRST_UNIT = (0, 0)
 W1_ON_SCALAR = (1, 1)
 
 
@@ -51,10 +51,10 @@ def tile_list_tyre_shear_features_kernel(
         nc.gpsimd.memset(xs_plane[:].bitcast(I32), 0)
         nc.vector.memset(tab_plane[:].bitcast(I32), 0)
 
-        warm_in = held([P, 1], F32, "warm_in")
-        warm_out = held([P, 1], F32, "warm_out")
-        nc.vector.memset(warm_in[:], 1.0)
-        nc.scalar.activation(warm_out[:], warm_in[:], ACT.Abs_reciprocal_sqrt)
+        one = held([P, 1], F32, "one")
+        nc.vector.memset(one[:], 1.0)
+        nc.scalar.activation(one[:], one[:], ACT.Abs_reciprocal_sqrt)
+        nc.scalar.activation(one[:], one[:], ACT.Sign)
 
         def load_quadrant(queue, plane, scales, quad):
             rows = scales[0, 4 * quad : 4 * quad + 4, :].bitcast(I32)
@@ -79,12 +79,12 @@ def tile_list_tyre_shear_features_kernel(
         tab_codes = [held([P, T], I32, "tab_codes%d" % a) for a in range(2)]
         nc.sync.dma_start(tab_codes[0][:], tab_words[0].rearrange("p t i -> p (t i)").bitcast(I32))
         nc.sync.dma_start(offsets[:], offs)
+        nc.sync.dma_start(tab_codes[1][:], tab_words[1].rearrange("p t i -> p (t i)").bitcast(I32))
         for quad in range(QUADS):
-            nc.gpsimd.dma_start(
+            nc.sync.dma_start(
                 tab_plane[32 * quad : 32 * quad + 8, :].bitcast(I32),
                 tab_scales[:, 4 * quad : 4 * quad + 4, :].bitcast(I32),
             )
-        nc.sync.dma_start(tab_codes[1][:], tab_words[1].rearrange("p t i -> p (t i)").bitcast(I32))
         nc.sync.dma_start(xs_codes[1][:], xs_rows[:, HALF:S])
 
         w1_raw = {}
@@ -132,17 +132,16 @@ def tile_list_tyre_shear_features_kernel(
                     stop=True,
                 )
                 offset, factor = fringe_col[:, b, t : t + 1], gain_col[:, b, t : t + 1]
-                on_vector = (b, h) == (0, 0) and t >= PACK - EARLY_ON_VECTOR
-                if on_vector:
+                if (b, h) == FIRST_UNIT:
                     nc.vector.tensor_scalar(r[:, t, :], bank[:], offset, factor, ALU.add, ALU.mult)
                 nc.scalar.activation(d[:, t, :], bank[:], ACT.Square, bias=offset)
-                if not on_vector:
+                if (b, h) != FIRST_UNIT:
                     nc.scalar.activation(
                         r[:, t, :], bank[:], ACT.Identity, bias=gain_fringe[:, b, t : t + 1], scale=factor
                     )
                 if (t + 1) % span == 0:
                     part = d[:, t + 1 - span : t + 1, :]
-                    nc.scalar.activation(part, part, ACT.Abs_reciprocal_sqrt, bias=1.0)
+                    nc.scalar.activation(part, part, ACT.Abs_reciprocal_sqrt, bias=one[:])
             damp[b, h], resp[b, h] = d, r
 
         def gather():

from contextlib import ExitStack

import concourse.mybir as mybir

K, K2, H, N, T, S = 1024, 512, 1024, 512, 2048, 1024
FLOPS = 2 * S * (K * H + K2 * H + H * N)

F32 = mybir.dt.float32
BF16 = mybir.dt.bfloat16
I32 = mybir.dt.int32
U32 = mybir.dt.uint32
U16 = mybir.dt.uint16
U8 = mybir.dt.uint8
FP8X4 = mybir.dt.float8_e4m3fn_x4
FP4X4 = mybir.dt.float4_e2m1fn_x4
ACT = mybir.ActivationFunctionType
ALU = mybir.AluOpType

P = 128
PACK = 4
PASS = P * PACK
QUADS = 4
HALF = S // 2
CHUNK = HALF // 2
CHUNKS = S // CHUNK
BANKS = 4
LAST_UNIT = (1, 1)
FIRST_UNIT = (0, 0)
W1_ON_SCALAR = (1, 1)


def tile_list_tyre_shear_features_kernel(
    tc, tab_words, tab_scales, offs, xs_words, xs_scales, w1, w2_words, w2_scales, fringe, gain, w3,
    out_0, out_1, out_2,
):
    nc = tc.nc
    with ExitStack() as ctx:
        keep = ctx.enter_context(tc.tile_pool(name="keep", bufs=1))
        ring = ctx.enter_context(tc.tile_pool(name="ring", bufs=2))
        psum = ctx.enter_context(tc.psum_pool(name="psum", bufs=1))

        def held(shape, dtype, name):
            return keep.tile(shape, dtype, name=name, align_bytes=64)

        offsets = keep.tile([P, S // 16], U16, name="offsets")

        w2_plane = held([P, H], U8, "w2_plane")
        xs_plane = held([P, S], U8, "xs_plane")
        tab_plane = held([P, T], U8, "tab_plane")
        nc.vector.memset(w2_plane[:].bitcast(I32), 0)
        nc.gpsimd.memset(xs_plane[:].bitcast(I32), 0)
        nc.vector.memset(tab_plane[:].bitcast(I32), 0)

        one = held([P, 1], F32, "one")
        nc.vector.memset(one[:], 1.0)
        nc.scalar.activation(one[:], one[:], ACT.Abs_reciprocal_sqrt)
        nc.scalar.activation(one[:], one[:], ACT.Sign)

        def load_quadrant(queue, plane, scales, quad):
            rows = scales[0, 4 * quad : 4 * quad + 4, :].bitcast(I32)
            queue.dma_start(plane[32 * quad : 32 * quad + 4, :].bitcast(I32), rows)

        for quad in range(QUADS):
            load_quadrant(nc.sync, w2_plane, w2_scales, quad)
        w2_raw = held([P, 2 * H], U8, "w2_raw")
        nc.sync.dma_start(w2_raw[:].bitcast(I32), w2_words[0].bitcast(I32))
        xs_codes = [held([P, HALF], I32, "xs_codes%d" % h) for h in range(2)]
        xs_rows = xs_words[0].rearrange("p c i -> p (c i)").bitcast(I32)
        nc.sync.dma_start(xs_codes[0][:], xs_rows[:, 0:HALF])
        for quad in range(QUADS):
            load_quadrant(nc.gpsimd if quad == QUADS - 1 else nc.sync, xs_plane, xs_scales, quad)
        fringe_col = held([P, 2, PACK], F32, "fringe_col")
        gain_col = held([P, 2, PACK], F32, "gain_col")
        gain_fringe = held([P, 2, PACK], F32, "gain_fringe")
        nc.sync.dma_start(fringe_col[:], fringe.rearrange("(b p t) -> p b t", b=2, t=PACK))
        nc.sync.dma_start(gain_col[:], gain.rearrange("(b p t) -> p b t", b=2, t=PACK))
        nc.vector.tensor_tensor(gain_fringe[:], gain_col[:], fringe_col[:], ALU.mult)

        tab_codes = [held([P, T], I32, "tab_codes%d" % a) for a in range(2)]
        nc.sync.dma_start(tab_codes[0][:], tab_words[0].rearrange("p t i -> p (t i)").bitcast(I32))
        nc.sync.dma_start(offsets[:], offs)
        nc.sync.dma_start(tab_codes[1][:], tab_words[1].rearrange("p t i -> p (t i)").bitcast(I32))
        for quad in range(QUADS):
            nc.sync.dma_start(
                tab_plane[32 * quad : 32 * quad + 8, :].bitcast(I32),
                tab_scales[:, 4 * quad : 4 * quad + 4, :].bitcast(I32),
            )
        nc.sync.dma_start(xs_codes[1][:], xs_rows[:, HALF:S])

        w1_raw = {}
        for b in range(2):
            for a in range(2):
                raw = held([P, PACK, PASS], F32, "w1_raw%d%d" % (b, a))
                rows = w1[PASS * a : PASS * (a + 1), PASS * b : PASS * (b + 1)]
                nc.sync.dma_start(raw[:], rows.rearrange("(p j) c -> p j c", j=PACK))
                w1_raw[b, a] = raw
        w3_raw = {}
        for b in range(2):
            raw = held([P, PACK, N], F32, "w3_raw%d" % b)
            nc.sync.dma_start(raw[:], w3[PASS * b : PASS * (b + 1), :].rearrange("(p j) c -> p j c", j=PACK))
            w3_raw[b] = raw

        w2_codes, w2_dealt = {}, {}
        for b in range(2):
            codes = held([P, 2 * PASS], U8, "w2_codes%d" % b)
            plane = held([P, PASS], U8, "w2_dealt%d" % b)
            code_dst = codes[:].rearrange("p (t q e) -> p q t e", t=PACK, e=2)
            code_src = w2_raw[:, 2 * PASS * b : 2 * PASS * (b + 1)].rearrange("p (q t e) -> p q t e", t=PACK, e=2)
            plane_dst = plane[:].rearrange("p (t q) -> p q t", t=PACK)
            plane_src = w2_plane[:, PASS * b : PASS * (b + 1)].rearrange("p (q t) -> p q t", t=PACK)
            for t in range(0, PACK, 2):
                nc.vector.tensor_copy(code_dst[:, :, t : t + 2, :], code_src[:, :, t : t + 2, :])
                nc.vector.tensor_copy(plane_dst[:, :, t : t + 2], plane_src[:, :, t : t + 2])
            w2_codes[b], w2_dealt[b] = codes, plane

        damp, resp = {}, {}

        def frame_terms(b, h):
            cols = slice(HALF * h, HALF * (h + 1))
            d = held([P, PACK, HALF], F32, "damp%d%d" % (b, h))
            r = held([P, PACK, HALF], F32, "resp%d%d" % (b, h))
            span = 2 if (b, h) == LAST_UNIT else PACK
            for t in range(PACK):
                bank = psum.tile([P, HALF], F32, name="frame_bank", tag="frame_bank", bufs=BANKS)
                nc.tensor.matmul_mx(
                    out=bank[:],
                    lhsT=w2_codes[b][:, 2 * P * t : 2 * P * (t + 1)].bitcast(FP4X4),
                    lhsT_scale=w2_dealt[b][:, P * t : P * (t + 1)],
                    rhs=xs_codes[h][:].bitcast(FP8X4),
                    rhs_scale=xs_plane[:, cols],
                    start=True,
                    stop=True,
                )
                offset, factor = fringe_col[:, b, t : t + 1], gain_col[:, b, t : t + 1]
                if (b, h) == FIRST_UNIT:
                    nc.vector.tensor_scalar(r[:, t, :], bank[:], offset, factor, ALU.add, ALU.mult)
                nc.scalar.activation(d[:, t, :], bank[:], ACT.Square, bias=offset)
                if (b, h) != FIRST_UNIT:
                    nc.scalar.activation(
                        r[:, t, :], bank[:], ACT.Identity, bias=gain_fringe[:, b, t : t + 1], scale=factor
                    )
                if (t + 1) % span == 0:
                    part = d[:, t + 1 - span : t + 1, :]
                    nc.scalar.activation(part, part, ACT.Abs_reciprocal_sqrt, bias=one[:])
            damp[b, h], resp[b, h] = d, r

        def gather():
            codes = [held([P, S], U32, "v_codes%d" % a) for a in range(2)]
            for a in range(2):
                nc.vector.tensor_copy(codes[a][:], tab_codes[a][:].bitcast(U32).indirect(offsets[:]))
            plane = held([P, S], U8, "v_plane")
            nc.vector.tensor_copy(plane[:], tab_plane[:].indirect(offsets[:]))
            return codes, plane

        def group_weight(raw, on_scalar):
            grouped = ring.tile([P, PACK * PASS], BF16, name="w_grouped", tag="w_grouped", bufs=4, align_bytes=64)
            dst = grouped[:].rearrange("p (t q j) -> p q j t", t=PACK, j=PACK)
            src = raw[:].rearrange("p j (q t) -> p q j t", t=PACK)
            copy = nc.scalar.copy if on_scalar else nc.vector.tensor_copy
            for t in range(0, PACK, 2):
                copy(dst[:, :, :, t : t + 2], src[:, :, :, t : t + 2])
            return grouped

        def quantise(grouped, width, name):
            codes = held([P, width], U32, name + "_codes")
            plane = held([P, width], U8, name + "_plane")
            nc.vector.quantize_mx(out=codes[:].bitcast(FP8X4), scales=plane[:], in_=grouped[:])
            return codes, plane

        w1_q, w3_q, z_q = {}, {}, {}

        def prepare_w1(b):
            grouped = [group_weight(w1_raw[b, a], (b, a) == W1_ON_SCALAR) for a in range(2)]
            for a in range(2):
                w1_q[b, a] = quantise(grouped[a], PASS, "w1_%d%d" % (b, a))

        def casing_bank(b, h, t):
            cols = slice(HALF * h, HALF * (h + 1))
            bank = psum.tile([P, HALF], F32, name="casing_bank", tag="casing_bank", bufs=BANKS)
            for a in range(2):
                codes, plane = w1_q[b, a]
                nc.tensor.matmul_mx(
                    out=bank[:],
                    lhsT=codes[:, P * t : P * (t + 1)].bitcast(FP8X4),
                    lhsT_scale=plane[:, P * t : P * (t + 1)],
                    rhs=v_codes[a][:, cols].bitcast(FP8X4),
                    rhs_scale=v_plane[4 * a : P, cols],
                    start=(a == 0),
                    stop=(a == 1),
                )
            return bank

        def finish_z(b, h, banks, start, width):
            cols = slice(start, start + width)
            d, r = damp[b, h], resp[b, h]
            for t in range(PACK):
                nc.vector.tensor_tensor(d[:, t, cols], banks[t][:, cols], d[:, t, cols], ALU.mult)
            grouped = ring.tile([P, PACK * width], BF16, name="z_grouped", tag="z_grouped", bufs=3, align_bytes=64)
            nc.vector.tensor_tensor(
                grouped[:].rearrange("p (c i t) -> p c t i", i=2, t=PACK),
                d[:, :, cols].rearrange("p t (c i) -> p c t i", i=2),
                r[:, :, cols].rearrange("p t (c i) -> p c t i", i=2),
                ALU.add,
            )
            codes, plane = quantise(grouped, width, "z_%d%d_%d" % (b, h, start))
            for first in range(0, width, CHUNK):
                chunk = (HALF * h + start + first) // CHUNK
                z_q[b, chunk] = (codes[:, first : first + CHUNK], plane[:, first : first + CHUNK])

        def casing_terms(b, h):
            banks = [casing_bank(b, h, t) for t in range(PACK)]
            width = CHUNK if (b, h) == LAST_UNIT else HALF
            for start in range(0, HALF, width):
                finish_z(b, h, banks, start, width)

        y_plane = held([P, S], U8, "y_plane")
        out_rows = out_0.rearrange("(p t) j -> p t j", t=PACK)
        out_words = out_1[0].rearrange("p m t -> p (m t)").bitcast(I32)

        def feature_pass(out, chunk, t, b):
            w_codes, w_plane = w3_q[b]
            z_codes, z_plane = z_q[b, chunk]
            nc.tensor.matmul_mx(
                out=out,
                lhsT=w_codes[:, P * t : P * (t + 1)].bitcast(FP8X4),
                lhsT_scale=w_plane[:, P * t : P * (t + 1)],
                rhs=z_codes.bitcast(FP8X4),
                rhs_scale=z_plane,
                start=(b == 0),
                stop=(b == 1),
            )

        def features(chunk):
            y = ring.tile([P, PACK, CHUNK], F32, name="y", tag="y", bufs=CHUNKS, align_bytes=64)
            if chunk < CHUNKS - 1:
                for u in range(0, PACK, 2):
                    bank = psum.tile([P, 2, CHUNK], F32, name="frame_bank", tag="frame_bank", bufs=BANKS)
                    for e in range(2):
                        for b in range(2):
                            feature_pass(bank[:, e, :], chunk, u + e, b)
                    nc.scalar.copy(y[:, u : u + 2, :], bank[:])
            else:
                banks = [
                    psum.tile([P, CHUNK], F32, name="casing_bank", tag="casing_bank", bufs=BANKS) for t in range(PACK)
                ]
                for b in range(2):
                    for t in range(PACK):
                        feature_pass(banks[t][:], chunk, t, b)
                for t in range(PACK):
                    copy = nc.vector.tensor_copy if t % 2 == 1 else nc.scalar.copy
                    copy(y[:, t, :], banks[t][:])
            nc.sync.dma_start(out_rows[:, :, CHUNK * chunk : CHUNK * (chunk + 1)], y[:])
            return y

        def group_features(chunk, y):
            grouped = ring.tile([P, PACK * CHUNK], BF16, name="y_grouped", tag="y_grouped", bufs=CHUNKS, align_bytes=64)
            copy = nc.scalar.copy if chunk < CHUNKS - 1 else nc.vector.tensor_copy
            copy(
                grouped[:].rearrange("p (c i t) -> p c t i", i=4, t=PACK),
                y[:].rearrange("p t (c i) -> p c t i", i=4),
            )
            return grouped

        def feature_planes(chunk, grouped):
            cols = slice(CHUNK * chunk, CHUNK * (chunk + 1))
            codes = held([P, CHUNK], U32, "y_codes%d" % chunk)
            nc.vector.quantize_mx(out=codes[:].bitcast(FP8X4), scales=y_plane[:, cols], in_=grouped[:])
            nc.sync.dma_start(out_words[:, cols], codes[:].bitcast(I32))

        frame_terms(0, 0)
        v_codes, v_plane = gather()
        prepare_w1(0)
        frame_terms(0, 1)
        casing_terms(0, 0)
        frame_terms(1, 0)
        prepare_w1(1)
        casing_terms(0, 1)
        w3_grouped = [group_weight(w3_raw[b], True) for b in range(2)]
        frame_terms(1, 1)
        casing_terms(1, 0)
        for b in range(2):
            w3_q[b] = quantise(w3_grouped[b], N, "w3_%d" % b)
        first_half = [group_features(chunk, features(chunk)) for chunk in range(CHUNKS // 2)]
        casing_terms(1, 1)
        second_half = [features(chunk) for chunk in range(CHUNKS // 2, CHUNKS)]
        for chunk in range(CHUNKS // 2):
            feature_planes(chunk, first_half[chunk])
        for chunk in range(CHUNKS // 2, CHUNKS):
            feature_planes(chunk, group_features(chunk, second_half[chunk - CHUNKS // 2]))
        for quad in range(QUADS):
            queue = nc.sync if quad % 2 == 0 else nc.scalar
            queue.dma_start(
                out_2[0, 4 * quad : 4 * quad + 4, :].bitcast(I32),
                y_plane[32 * quad : 32 * quad + 4, :].bitcast(I32),
            )
